import numpy as np
import ml_dtypes


def mxq(x, axis, fmt="e4m3"):
    dtype, down = {"e4m3": (ml_dtypes.float8_e4m3fn, 7), "e5m2": (ml_dtypes.float8_e5m2, 14)}[fmt]
    v = np.moveaxis(np.asarray(x, np.float32).astype(ml_dtypes.bfloat16).astype(np.float64), axis, -1)
    blocks = v.reshape(v.shape[:-1] + (-1, 32))
    amax = np.abs(blocks).max(-1, keepdims=True)
    byte = np.maximum(np.where(amax > 0, np.frexp(amax)[1] - 1 + 127, 0) - down, 1)
    scale = np.exp2(byte - 127.0)
    codes = (blocks / scale).astype(np.float32).astype(dtype).astype(np.float64)
    return np.moveaxis((codes * scale).reshape(v.shape), -1, axis)


WIDE = False


def mx_kscale(k):
    if not WIDE:
        return np.ones(k)
    levels = np.array([10, -10, 5, -5, 0])
    if k % 512:
        return np.exp2(np.random.permutation(np.resize(levels, k // 32))).repeat(32)
    a = np.empty((k // 512, 16))
    for p in range(k // 512):
        a[p, :8] = np.random.permutation(np.resize(levels, 8))
        for g in range(8):
            far = levels[np.abs(levels - a[p, g]) >= 10]
            a[p, g + 8] = far[np.random.randint(len(far))]
    return np.exp2(a.ravel()).repeat(32)


def f64(x):
    return np.asarray(x).astype(np.float64)


def striped(idx):
    return np.tile(idx.reshape(-1, 16).T, (8, 1)).astype(np.uint16)


def unstriped(offs):
    return offs[:16].T.reshape(-1).astype(np.int64)


def pack_weight(w):
    k, n = w.shape
    w = f64(np.asarray(w, np.float32).astype(ml_dtypes.bfloat16)).reshape(k // 32, 32, n)
    amax = np.abs(w).max(1)
    byte = np.clip(np.where(amax > 0, np.frexp(amax)[1] - 1 + 127 - 7, 1), 1, 254)
    scaled = (w * np.exp2(127.0 - byte)[:, None, :]).reshape(k, n).astype(np.float32)
    words = np.ascontiguousarray(scaled.reshape(k // 512, 128, 4, n).transpose(0, 1, 3, 2)).astype(ml_dtypes.float8_e4m3fn).view(np.uint8)
    return words, np.ascontiguousarray(byte.astype(np.uint8).reshape(k // 512, 16, n))


def unpack_weight(words, scales):
    g, p, n, _ = words.shape
    vals = np.ascontiguousarray(words).view(ml_dtypes.float8_e4m3fn).astype(np.float64) * np.repeat(np.exp2(scales.astype(np.float64) - 127.0), 8, axis=1)[..., None]
    return vals.transpose(0, 1, 3, 2).reshape(g * 512, n)


E2M1 = np.array([0.0, 0.5, 1.0, 1.5, 2.0, 3.0, 4.0, 6.0, -0.0, -0.5, -1.0, -1.5, -2.0, -3.0, -4.0, -6.0])


def pack_fp4(w):
    k, n = w.shape
    w = f64(np.asarray(w, np.float32).astype(ml_dtypes.bfloat16)).reshape(k // 32, 32, n)
    amax = np.abs(w).max(1)
    mant, ex = np.frexp(amax / 6.0)
    byte = np.clip(np.where(amax > 0, np.where(mant > 0.5, ex, ex - 1) + 127, 1), 1, 254)
    scaled = (w * np.exp2(127.0 - byte)[:, None, :]).reshape(k, n).astype(np.float32)
    c = np.ascontiguousarray(scaled.reshape(k // 512, 128, 4, n).transpose(0, 1, 3, 2)).astype(ml_dtypes.float4_e2m1fn).view(np.uint8) & 0xF
    words = (c[..., 0::2] | (c[..., 1::2] << 4)).reshape(k // 512, 128, 2 * n)
    return np.ascontiguousarray(words), np.ascontiguousarray(byte.astype(np.uint8).reshape(k // 512, 16, n))


def unpack_fp4(words, scales):
    g, _, n = scales.shape
    words = np.ascontiguousarray(words).reshape(g, 128, n, 2)
    nib = np.empty((g, 128, n, 4), np.uint8)
    nib[..., 0::2] = words & 0xF
    nib[..., 1::2] = words >> 4
    vals = E2M1[nib] * np.repeat(np.exp2(scales.astype(np.float64) - 127.0), 8, axis=1)[..., None]
    return vals.transpose(0, 1, 3, 2).reshape(g * 512, n)


def sigmoid(v):
    return 1.0 / (1.0 + np.exp(-np.maximum(v, -700.0)))

def planes(y):
    n, m = y.shape
    v = y.astype(np.float32).astype(ml_dtypes.bfloat16).astype(np.float64).reshape(n // 32, 32, m)
    top = np.abs(v).max(1)
    byte = np.clip(np.where(top > 0, np.frexp(top)[1] - 1 + 127 - 7, 1), 1, 254)
    codes = (v * np.exp2(127.0 - byte)[:, None, :]).reshape(n, m).astype(np.float32).astype(ml_dtypes.float8_e4m3fn).view(np.uint8)
    words = codes.reshape(n // 512, 128, 4, m).transpose(0, 1, 3, 2)
    return np.ascontiguousarray(words), np.ascontiguousarray(byte.astype(np.uint8).reshape(n // 512, 16, m))


K, T, S, N, H, W = 512, 2048, 256, 512, 512, 1024


def setup_inputs():
    n = np.random.standard_normal
    s = mx_kscale(K)[:, None]
    u = mx_kscale(H)
    packed_xT = pack_weight(n((K, T)) * s)
    packed_w1 = pack_fp4(n((K, H)) / np.sqrt(K) / s)
    packed_w2 = pack_fp4(n((K, H)) / np.sqrt(K) / s)
    packed_w3 = pack_fp4(n((H, N)) / np.sqrt(H) / u[:, None])
    return {
        "x_words": packed_xT[0],
        "x_scales": packed_xT[1],
        "w1_words": packed_w1[0],
        "w1_scales": packed_w1[1],
        "w2_words": packed_w2[0],
        "w2_scales": packed_w2[1],
        "gn": (np.random.uniform(0.5, 1.5, (H, 1)) * u[:, None]).astype(np.float32),
        "w3_words": packed_w3[0],
        "w3_scales": packed_w3[1],
        "offs": striped(np.random.permutation(T)[:S]),
        "two": striped(np.random.permutation(T)[:S]),
        "n1": striped(np.random.permutation(S)),
        "n2": striped(np.random.permutation(S)),
        "n3": striped(np.random.permutation(S)),
        "n4": striped(np.random.randint(0, S, W)),
    }


def reference(x_words, x_scales, w1_words, w1_scales, w2_words, w2_scales, gn, w3_words, w3_scales, offs, two, n1, n2, n3, n4):
    x_two = unpack_weight(x_words, x_scales)[:, unstriped(two)]
    d = unpack_fp4(w2_words, w2_scales).T @ x_two
    xq = unpack_weight(x_words, x_scales)[:, unstriped(offs)]
    y = unpack_fp4(w1_words, w1_scales).T @ xq
    z = f64(gn) * (d * (y[:, unstriped(n1)] - y) + 0.5 * (d[:, unstriped(n3)] * (y[:, unstriped(n2)] - y)))
    h = unpack_fp4(w3_words, w3_scales).T @ mxq(z, 0, "e4m3")
    mb = h[:, unstriped(n4)]
    ms = mb.reshape(N, S, 4).sum(axis=2)
    out_0 = h * sigmoid(ms)
    return (out_0,) + planes(out_0)

@@ -1,0 +1,326 @@
+from contextlib import ExitStack
+
+import concourse.mybir as mybir
+
+F32 = mybir.dt.float32
+BF16 = mybir.dt.bfloat16
+I32 = mybir.dt.int32
+U32 = mybir.dt.uint32
+U16 = mybir.dt.uint16
+U8 = mybir.dt.uint8
+FP8X4 = mybir.dt.float8_e4m3fn_x4
+FP4X4 = mybir.dt.float4_e2m1fn_x4
+MULT = mybir.AluOpType.mult
+ADD = mybir.AluOpType.add
+SUBTRACT = mybir.AluOpType.subtract
+COPY = mybir.ActivationFunctionType.Copy
+SIGMOID = mybir.ActivationFunctionType.Sigmoid
+
+P = 128
+PACK = 4
+T = 2048
+S = 256
+HALF = S // 2
+FEATURES = P * PACK
+MEMBERS = 4
+LIST_ROWS = 16
+SPARE = 16
+FLOPS = 3 * 2 * FEATURES * FEATURES * S
+
+CHUNKS = ((0, 64), (64, 128), (128, 192), (192, 224), (224, 256))
+QUANT_GROUPS = ((0, 128), (128, 192), (192, 256))
+VECTOR_GATHERS = (2, 2, 1, 0, 0)
+
+
+def load_scale_rows(queue, plane, scales):
+    for q in range(4):
+        queue.dma_start(plane[32 * q : 32 * q + 4, :].bitcast(I32), scales[0, 4 * q : 4 * q + 4, :].bitcast(I32))
+
+
+def interleave(copy, grouped, rows):
+    copy(
+        grouped.rearrange("p (c i) t -> p c t i", i=4),
+        rows.rearrange("p t (c i) -> p c t i", i=4),
+    )
+
+
+def tile_picked_twlflowbgsumg_none_po_kernel(
+    tc, x_words, x_scales, w1_words, w1_scales, w2_words, w2_scales, gn, w3_words, w3_scales,
+    offs, two, n1, n2, n3, n4, out_0, out_1, out_2,
+):
+    nc = tc.nc
+    with ExitStack() as ctx:
+        keep = ctx.enter_context(tc.tile_pool(name="keep", bufs=1))
+        psum = ctx.enter_context(tc.psum_pool(name="psum", bufs=8))
+
+        def sbuf(name, shape, dtype, tag=None):
+            return keep.tile(shape, dtype, name=name, tag=tag or name, align_bytes=64)
+
+        def bank(name):
+            return psum.tile([P, 512], F32, name=name, tag="bank")
+
+        def load_list(name, source):
+            tile = sbuf(name, list(source.shape), U16)
+            nc.sync.dma_start(tile[:], source)
+            return tile
+
+        def zeroed_plane(name, width):
+            plane = sbuf(name, [P, width], U8)
+            nc.vector.memset(plane[:].bitcast(I32), 0)
+            return plane
+
+        def load_words(name, words, queue, tag=None):
+            raw = sbuf(name, [P, 2 * FEATURES], U8, tag)
+            queue.dma_start(raw[:].bitcast(I32), words[0].bitcast(I32))
+            return raw
+
+        def deal_words(name, raw, tag=None):
+            dealt = sbuf(name, [P, 2 * FEATURES], U8, tag)
+            nc.vector.tensor_copy(
+                dealt[:].rearrange("p (t m b) -> p t m b", t=PACK, b=2),
+                raw[:].rearrange("p (m t b) -> p t m b", t=PACK, b=2),
+            )
+            return dealt
+
+        def deal_scales(name, raw, tag=None):
+            dealt = sbuf(name, [P, FEATURES], U8, tag)
+            nc.vector.tensor_copy(
+                dealt[:].rearrange("p (t m) -> p t m", t=PACK),
+                raw[:].rearrange("p (m t) -> p t m", t=PACK),
+            )
+            return dealt
+
+        def window(name):
+            tile = sbuf(name, [P, S + SPARE], F32)
+            nc.gpsimd.memset(tile[:, S:], 0.0)
+            return tile
+
+        def product(out, words, scales, t, codes, code_scales):
+            nc.tensor.matmul_mx(
+                out,
+                lhsT=words[:, 2 * P * t : 2 * P * (t + 1)].bitcast(FP4X4),
+                lhsT_scale=scales[:, P * t : P * (t + 1)],
+                rhs=codes.bitcast(FP8X4),
+                rhs_scale=code_scales,
+                start=True,
+                stop=True,
+            )
+
+        w1_plane = zeroed_plane("w1_plane", FEATURES)
+        x_plane = zeroed_plane("x_plane", T)
+        w2_plane = zeroed_plane("w2_plane", FEATURES)
+        w1_raw = load_words("w1_raw", w1_words, nc.sync)
+        load_scale_rows(nc.scalar, w1_plane, w1_scales)
+        x_table = sbuf("x_table", [P, T], U32)
+        nc.sync.dma_start(x_table[:].bitcast(I32), x_words[0].rearrange("p c r -> p (c r)").bitcast(I32))
+        offs_t = load_list("offs_t", offs)
+        two_t = load_list("two_t", two)
+        load_scale_rows(nc.sync, x_plane, x_scales)
+        load_scale_rows(nc.sync, w2_plane, w2_scales)
+        w2_raw = load_words("w2_raw", w2_words, nc.gpsimd)
+        gain = sbuf("gain", [P, PACK], F32)
+        nc.gpsimd.dma_start(gain[:], gn.rearrange("(p t) o -> p (t o)", t=PACK))
+        n1_t = load_list("n1_t", n1)
+        n2_t = load_list("n2_t", n2)
+        n3_t = load_list("n3_t", n3)
+        n4_t = load_list("n4_t", n4)
+
+        y_rows = [window(f"y_rows{t}") for t in range(PACK)]
+        d_rows = [window(f"d_rows{t}") for t in range(PACK)]
+        h_rows = [window(f"h_rows{t}") for t in range(PACK)]
+
+        w1_dealt = deal_words("w1_dealt", w1_raw)
+        w1_sdealt = deal_scales("w1_sdealt", w1_plane)
+        w2_dealt = deal_words("w2_dealt", w2_raw)
+        w3_raw = load_words("w3_raw", w3_words, nc.sync, "w1_raw")
+        load_scale_rows(nc.sync, w1_plane, w3_scales)
+
+        def pick(name, offsets):
+            codes = sbuf(name + "_codes", [P, S], U32)
+            code_scales = sbuf(name + "_scales", [P, S], U8)
+            nc.vector.tensor_copy(codes[:], x_table[:].indirect(offsets[:]))
+            nc.vector.tensor_copy(code_scales[:], x_plane[:].indirect(offsets[:]))
+            return codes, code_scales
+
+        xq_codes, xq_scales = pick("xq", offs_t)
+        w2_sdealt = deal_scales("w2_sdealt", w2_plane)
+        x2_codes, x2_scales = pick("x2", two_t)
+
+        banks = [bank(f"yd_bank{t}") for t in range(PACK + 1)]
+        y_sums = [banks[t][:, :S] for t in range(PACK)]
+        d_sums = [banks[t + 1][:, S:] for t in range(PACK)]
+        for t in range(PACK):
+            product(y_sums[t], w1_dealt, w1_sdealt, t, xq_codes[:], xq_scales[:])
+        for t in range(PACK):
+            product(d_sums[t], w2_dealt, w2_sdealt, t, x2_codes[:], x2_scales[:])
+        w3_sdealt = deal_scales("w3_sdealt", w1_plane, "x_plane")
+
+        z_rows = sbuf("z_rows", [P, 2, PACK, HALF], F32)
+        pieces = [(t, 0, S) for t in range(PACK - 1)] + [(PACK - 1, 0, HALF), (PACK - 1, HALF, S)]
+        fetched, steps, first, second, d_fetched = {}, {}, {}, {}, {}
+
+        def entries(offsets, c0, c1):
+            return offsets[:, c0 // LIST_ROWS : c1 // LIST_ROWS]
+
+        def y_out(t):
+            nc.scalar.activation(y_rows[t][:, :S], y_sums[t], COPY, scale=gain[:, t : t + 1])
+
+        def d_out(t):
+            nc.scalar.copy(d_rows[t][:, :S], d_sums[t])
+
+        def fetch_y(i):
+            t, c0, c1 = pieces[i]
+            fetched[i] = sbuf(f"fetched{i}", [P, 2, c1 - c0], F32)
+            nc.scalar.activation(fetched[i][:, 0, :], y_rows[t][:].indirect(entries(n1_t, c0, c1)), COPY)
+            nc.scalar.activation(fetched[i][:, 1, :], y_rows[t][:].indirect(entries(n2_t, c0, c1)), COPY)
+
+        def fetch_d(i):
+            t, c0, c1 = pieces[i]
+            d_fetched[i] = sbuf(f"d_fetched{i}", [P, c1 - c0], F32)
+            nc.scalar.activation(d_fetched[i][:], d_rows[t][:].indirect(entries(n3_t, c0, c1)), COPY)
+
+        def differences(i):
+            t, c0, c1 = pieces[i]
+            steps[i] = sbuf(f"steps{i}", [P, 2, c1 - c0], F32)
+            here = y_rows[t][:, c0:c1].unsqueeze(1).to_broadcast([P, 2, c1 - c0])
+            nc.vector.tensor_tensor(steps[i][:], fetched[i][:], here, SUBTRACT)
+
+        def terms(i):
+            t, c0, c1 = pieces[i]
+            first[i] = sbuf(f"first{i}", [P, c1 - c0], F32)
+            second[i] = sbuf(f"second{i}", [P, c1 - c0], F32)
+            d_there = d_fetched[i][:] if i in d_fetched else d_rows[t][:].indirect(entries(n3_t, c0, c1))
+            nc.vector.tensor_tensor(first[i][:], d_rows[t][:, c0:c1], steps[i][:, 0, :], MULT)
+            nc.vector.tensor_tensor(second[i][:], d_there, steps[i][:, 1, :], MULT)
+
+        def join(i):
+            t, c0, c1 = pieces[i]
+            nc.vector.scalar_tensor_tensor(
+                z_rows[:, c0 // HALF : c1 // HALF, t, :],
+                second[i][:].rearrange("p (u c) -> p u c", c=HALF),
+                0.5,
+                first[i][:].rearrange("p (u c) -> p u c", c=HALF),
+                MULT,
+                ADD,
+            )
+
+        y_out(0)
+        fetch_y(0)
+        d_out(0)
+        differences(0)
+        w3_dealt = deal_words("w3_dealt", w3_raw, "x_table")
+        for i in range(1, len(pieces)):
+            t, c0, c1 = pieces[i]
+            if c0 == 0:
+                y_out(t)
+                d_out(t)
+            fetch_y(i)
+            if t == PACK - 1:
+                fetch_d(i)
+            terms(i - 1)
+            differences(i)
+            join(i - 1)
+        terms(len(pieces) - 1)
+
+        z_grouped = [sbuf(f"z_grouped{u}", [P, HALF, PACK], BF16) for u in range(2)]
+        h_banks = {}
+
+        def last_layer(u):
+            codes = sbuf(f"z_codes{u}", [P, HALF], U32)
+            code_scales = sbuf(f"z_scales{u}", [P, HALF], U8)
+            nc.vector.quantize_mx(codes[:].bitcast(FP8X4), code_scales[:], z_grouped[u][:].rearrange("p c t -> p (c t)"))
+            for pair in range(2):
+                h_banks[u, pair] = bank(f"h_bank{u}_{pair}")
+                for t in (2 * pair, 2 * pair + 1):
+                    product(h_banks[u, pair][:, HALF * (t % 2) : HALF * (t % 2 + 1)], w3_dealt, w3_sdealt, t, codes[:], code_scales[:])
+            for t in range(PACK):
+                copy = nc.vector.tensor_copy if u == 1 and t < 2 else nc.scalar.copy
+                copy(h_rows[t][:, HALF * u : HALF * (u + 1)], h_banks[u, t // 2][:, HALF * (t % 2) : HALF * (t % 2 + 1)])
+
+        interleave(nc.scalar.copy, z_grouped[0][:], z_rows[:, 0])
+        join(len(pieces) - 1)
+        last_layer(0)
+        interleave(nc.vector.tensor_copy, z_grouped[1][:], z_rows[:, 1])
+        last_layer(1)
+
+        out_rows = out_0.rearrange("(p t) c -> p t c", t=PACK)
+        out_words = out_1[0].rearrange("p c r -> p (c r)").bitcast(I32)
+        out_plane = sbuf("out_plane", [P, S], U8)
+        results = {g0: sbuf(f"result{g0}", [P, PACK, g1 - g0], F32) for g0, g1 in QUANT_GROUPS}
+        grouped = {g0: sbuf(f"out_grouped{g0}", [P, g1 - g0, PACK], BF16) for g0, g1 in QUANT_GROUPS}
+        members, pairs, sums, gates = {}, {}, {}, {}
+
+        def fetch_members(k):
+            c0, c1 = CHUNKS[k]
+            members[k] = sbuf(f"members{k}", [P, PACK, MEMBERS * (c1 - c0)], F32)
+            for t in range(PACK):
+                looked_up = h_rows[t][:].indirect(entries(n4_t, MEMBERS * c0, MEMBERS * c1))
+                if t < VECTOR_GATHERS[k]:
+                    nc.vector.tensor_copy(members[k][:, t, :], looked_up)
+                else:
+                    nc.scalar.activation(members[k][:, t, :], looked_up, COPY)
+
+        def add_pairs(k):
+            c0, c1 = CHUNKS[k]
+            fours = members[k][:].rearrange("p t (c f) -> p (t c) f", f=MEMBERS)
+            pairs[k] = sbuf(f"pairs{k}", [P, PACK * (c1 - c0), 2], F32)
+            nc.vector.tensor_tensor(pairs[k][:], fours[:, :, 0:2], fours[:, :, 2:4], ADD)
+
+        def gate(k):
+            c0, c1 = CHUNKS[k]
+            sums[k] = sbuf(f"sums{k}", [P, PACK * (c1 - c0)], F32)
+            gates[k] = sbuf(f"gates{k}", [P, PACK, c1 - c0], F32)
+            nc.vector.tensor_tensor(sums[k][:], pairs[k][:, :, 0], pairs[k][:, :, 1], ADD)
+            nc.scalar.activation(gates[k][:].rearrange("p t c -> p (t c)"), sums[k][:], SIGMOID)
+
+        def group_of(k):
+            return [g for g in QUANT_GROUPS if g[0] <= CHUNKS[k][0] < g[1]][0]
+
+        def multiply(k):
+            c0, c1 = CHUNKS[k]
+            g0, g1 = group_of(k)
+            u = c0 // HALF
+            for pair in range(2):
+                h_here = h_banks[u, pair][:, :S].rearrange("p (t c) -> p t c", t=2)
+                nc.vector.tensor_tensor(
+                    results[g0][:, 2 * pair : 2 * pair + 2, c0 - g0 : c1 - g0],
+                    h_here[:, :, c0 - HALF * u : c1 - HALF * u],
+                    gates[k][:, 2 * pair : 2 * pair + 2, :],
+                    MULT,
+                )
+            if c1 == g1:
+                nc.sync.dma_start(out_rows[:, :, g0:g1], results[g0][:])
+
+        def regroup(k):
+            g0, g1 = group_of(k)
+            if CHUNKS[k][1] == g1:
+                interleave(nc.vector.tensor_copy, grouped[g0][:], results[g0][:])
+
+        def quantise(k):
+            g0, g1 = group_of(k)
+            if CHUNKS[k][1] == g1:
+                codes = sbuf(f"out_codes{g0}", [P, g1 - g0], U32)
+                nc.vector.quantize_mx(codes[:].bitcast(FP8X4), out_plane[:, g0:g1], grouped[g0][:].rearrange("p c t -> p (c t)"))
+                nc.sync.dma_start(out_words[:, g0:g1], codes[:].bitcast(I32))
+
+        last = len(CHUNKS) - 1
+        fetch_members(0)
+        fetch_members(1)
+        for k in range(len(CHUNKS)):
+            add_pairs(k)
+            if k >= 2:
+                quantise(k - 2)
+            if k + 2 <= last:
+                fetch_members(k + 2)
+            if k >= 1:
+                multiply(k - 1)
+            gate(k)
+            if k >= 1:
+                regroup(k - 1)
+        quantise(last - 1)
+        multiply(last)
+        regroup(last)
+        quantise(last)
+        for q in range(4):
+            queue = nc.scalar if q % 2 else nc.sync
+            queue.dma_start(out_2[0, 4 * q : 4 * q + 4, :].bitcast(I32), out_plane[32 * q : 32 * q + 4, :].bitcast(I32))

@@ -32,8 +32,8 @@ QUANT_GROUPS = ((0, 128), (128, 192), (192, 256))
 VECTOR_GATHERS = (2, 2, 1, 0, 0)
 
 
-def load_scale_rows(queue, plane, scales):
-    for q in range(4):
+def load_scale_rows(queues, plane, scales):
+    for q, queue in enumerate(queues):
         queue.dma_start(plane[32 * q : 32 * q + 4, :].bitcast(I32), scales[0, 4 * q : 4 * q + 4, :].bitcast(I32))
 
 
@@ -92,7 +92,7 @@ def tile_picked_twlflowbgsumg_none_po_kernel(
 
         def window(name):
             tile = sbuf(name, [P, S + SPARE], F32)
-            nc.gpsimd.memset(tile[:, S:], 0.0)
+            nc.vector.memset(tile[:, S:], 0.0)
             return tile
 
         def product(out, words, scales, t, codes, code_scales):
@@ -106,24 +106,28 @@ def tile_picked_twlflowbgsumg_none_po_kernel(
                 stop=True,
             )
 
+        warm_in = sbuf("warm_in", [P, 1], F32)
+        warm_out = sbuf("warm_out", [P, 1], F32)
+        nc.gpsimd.memset(warm_in[:], 0.0)
+        nc.scalar.activation(warm_out[:], warm_in[:], SIGMOID)
         w1_plane = zeroed_plane("w1_plane", FEATURES)
         x_plane = zeroed_plane("x_plane", T)
         w2_plane = zeroed_plane("w2_plane", FEATURES)
         w1_raw = load_words("w1_raw", w1_words, nc.sync)
-        load_scale_rows(nc.scalar, w1_plane, w1_scales)
-        x_table = sbuf("x_table", [P, T], U32)
-        nc.sync.dma_start(x_table[:].bitcast(I32), x_words[0].rearrange("p c r -> p (c r)").bitcast(I32))
         offs_t = load_list("offs_t", offs)
         two_t = load_list("two_t", two)
-        load_scale_rows(nc.sync, x_plane, x_scales)
-        load_scale_rows(nc.sync, w2_plane, w2_scales)
-        w2_raw = load_words("w2_raw", w2_words, nc.gpsimd)
-        gain = sbuf("gain", [P, PACK], F32)
-        nc.gpsimd.dma_start(gain[:], gn.rearrange("(p t) o -> p (t o)", t=PACK))
         n1_t = load_list("n1_t", n1)
         n2_t = load_list("n2_t", n2)
         n3_t = load_list("n3_t", n3)
         n4_t = load_list("n4_t", n4)
+        x_table = sbuf("x_table", [P, T], U32)
+        nc.sync.dma_start(x_table[:].bitcast(I32), x_words[0].rearrange("p c r -> p (c r)").bitcast(I32))
+        load_scale_rows([nc.scalar] * 3 + [nc.gpsimd], w1_plane, w1_scales)
+        load_scale_rows([nc.scalar] * 4, x_plane, x_scales)
+        load_scale_rows([nc.scalar] * 4, w2_plane, w2_scales)
+        w2_raw = load_words("w2_raw", w2_words, nc.gpsimd)
+        gain = sbuf("gain", [P, PACK], F32)
+        nc.gpsimd.dma_start(gain[:], gn.rearrange("(p t) o -> p (t o)", t=PACK))
 
         y_rows = [window(f"y_rows{t}") for t in range(PACK)]
         d_rows = [window(f"d_rows{t}") for t in range(PACK)]
@@ -133,7 +137,7 @@ def tile_picked_twlflowbgsumg_none_po_kernel(
         w1_sdealt = deal_scales("w1_sdealt", w1_plane)
         w2_dealt = deal_words("w2_dealt", w2_raw)
         w3_raw = load_words("w3_raw", w3_words, nc.sync, "w1_raw")
-        load_scale_rows(nc.sync, w1_plane, w3_scales)
+        load_scale_rows([nc.sync] * 4, w1_plane, w3_scales)
 
         def pick(name, offsets):
             codes = sbuf(name + "_codes", [P, S], U32)
@@ -153,11 +157,11 @@ def tile_picked_twlflowbgsumg_none_po_kernel(
             product(y_sums[t], w1_dealt, w1_sdealt, t, xq_codes[:], xq_scales[:])
         for t in range(PACK):
             product(d_sums[t], w2_dealt, w2_sdealt, t, x2_codes[:], x2_scales[:])
-        w3_sdealt = deal_scales("w3_sdealt", w1_plane, "x_plane")
 
-        z_rows = sbuf("z_rows", [P, 2, PACK, HALF], F32)
+        first = sbuf("first", [P, PACK, S], F32)
+        second = sbuf("second", [P, PACK, S], F32)
         pieces = [(t, 0, S) for t in range(PACK - 1)] + [(PACK - 1, 0, HALF), (PACK - 1, HALF, S)]
-        fetched, steps, first, second, d_fetched = {}, {}, {}, {}, {}
+        fetched, steps, d_fetched = {}, {}, {}
 
         def entries(offsets, c0, c1):
             return offsets[:, c0 // LIST_ROWS : c1 // LIST_ROWS]
@@ -166,7 +170,7 @@ def tile_picked_twlflowbgsumg_none_po_kernel(
             nc.scalar.activation(y_rows[t][:, :S], y_sums[t], COPY, scale=gain[:, t : t + 1])
 
         def d_out(t):
-            nc.scalar.copy(d_rows[t][:, :S], d_sums[t])
+            nc.scalar.activation(d_rows[t][:, :S], d_sums[t], COPY, scale=0.5)
 
         def fetch_y(i):
             t, c0, c1 = pieces[i]
@@ -185,22 +189,23 @@ def tile_picked_twlflowbgsumg_none_po_kernel(
             here = y_rows[t][:, c0:c1].unsqueeze(1).to_broadcast([P, 2, c1 - c0])
             nc.vector.tensor_tensor(steps[i][:], fetched[i][:], here, SUBTRACT)
 
-        def terms(i):
+        def first_term(i):
             t, c0, c1 = pieces[i]
-            first[i] = sbuf(f"first{i}", [P, c1 - c0], F32)
-            second[i] = sbuf(f"second{i}", [P, c1 - c0], F32)
-            d_there = d_fetched[i][:] if i in d_fetched else d_rows[t][:].indirect(entries(n3_t, c0, c1))
-            nc.vector.tensor_tensor(first[i][:], d_rows[t][:, c0:c1], steps[i][:, 0, :], MULT)
-            nc.vector.tensor_tensor(second[i][:], d_there, steps[i][:, 1, :], MULT)
+            nc.vector.scalar_tensor_tensor(first[:, t, c0:c1], steps[i][:, 0, :], 2.0, d_rows[t][:, c0:c1], MULT, MULT)
 
-        def join(i):
+        def second_term(i):
             t, c0, c1 = pieces[i]
-            nc.vector.scalar_tensor_tensor(
-                z_rows[:, c0 // HALF : c1 // HALF, t, :],
-                second[i][:].rearrange("p (u c) -> p u c", c=HALF),
-                0.5,
-                first[i][:].rearrange("p (u c) -> p u c", c=HALF),
-                MULT,
+            d_there = d_fetched[i][:] if i in d_fetched else d_rows[t][:].indirect(entries(n3_t, c0, c1))
+            nc.vector.tensor_tensor(second[:, t, c0:c1], d_there, steps[i][:, 1, :], MULT)
+
+        z_grouped = [sbuf(f"z_grouped{u}", [P, HALF, PACK], BF16) for u in range(2)]
+
+        def join(u):
+            cols = slice(HALF * u, HALF * (u + 1))
+            nc.vector.tensor_tensor(
+                z_grouped[u][:].rearrange("p (c i) t -> p c t i", i=4),
+                first[:, :, cols].rearrange("p t (c i) -> p c t i", i=4),
+                second[:, :, cols].rearrange("p t (c i) -> p c t i", i=4),
                 ADD,
             )
 
@@ -208,7 +213,7 @@ def tile_picked_twlflowbgsumg_none_po_kernel(
         fetch_y(0)
         d_out(0)
         differences(0)
-        w3_dealt = deal_words("w3_dealt", w3_raw, "x_table")
+        w3_dealt = deal_words("w3_dealt", w3_raw, "fetched0")
         for i in range(1, len(pieces)):
             t, c0, c1 = pieces[i]
             if c0 == 0:
@@ -217,12 +222,12 @@ def tile_picked_twlflowbgsumg_none_po_kernel(
             fetch_y(i)
             if t == PACK - 1:
                 fetch_d(i)
-            terms(i - 1)
+            first_term(i - 1)
+            second_term(i - 1)
             differences(i)
-            join(i - 1)
-        terms(len(pieces) - 1)
+            if i == 1:
+                w3_sdealt = deal_scales("w3_sdealt", w1_plane, "fetched1")
 
-        z_grouped = [sbuf(f"z_grouped{u}", [P, HALF, PACK], BF16) for u in range(2)]
         h_banks = {}
 
         def last_layer(u):
@@ -237,10 +242,11 @@ def tile_picked_twlflowbgsumg_none_po_kernel(
                 copy = nc.vector.tensor_copy if u == 1 and t < 2 else nc.scalar.copy
                 copy(h_rows[t][:, HALF * u : HALF * (u + 1)], h_banks[u, t // 2][:, HALF * (t % 2) : HALF * (t % 2 + 1)])
 
-        interleave(nc.scalar.copy, z_grouped[0][:], z_rows[:, 0])
-        join(len(pieces) - 1)
+        join(0)
+        first_term(len(pieces) - 1)
+        second_term(len(pieces) - 1)
         last_layer(0)
-        interleave(nc.vector.tensor_copy, z_grouped[1][:], z_rows[:, 1])
+        join(1)
         last_layer(1)
 
         out_rows = out_0.rearrange("(p t) c -> p t c", t=PACK)

@@ -30,11 +30,12 @@ FLOPS = 3 * 2 * FEATURES * FEATURES * S
 CHUNKS = ((0, 64), (64, 128), (128, 192), (192, 224), (224, 256))
 QUANT_GROUPS = ((0, 128), (128, 192), (192, 256))
 VECTOR_GATHERS = (2, 2, 1, 0, 0)
+BANK_TILES = (((0, 4),), ((0, 2), (2, 4)))
 
 
 def load_scale_rows(queues, plane, scales):
     for q, queue in enumerate(queues):
-        queue.dma_start(plane[32 * q : 32 * q + 4, :].bitcast(I32), scales[0, 4 * q : 4 * q + 4, :].bitcast(I32))
+        queue.dma_start(plane[32 * q : 32 * q + 4, :].bitcast(I32), scales[4 * q : 4 * q + 4, :].bitcast(I32))
 
 
 def interleave(copy, grouped, rows):
@@ -69,16 +70,14 @@ def tile_picked_twlflowbgsumg_none_po_kernel(
             nc.vector.memset(plane[:].bitcast(I32), 0)
             return plane
 
-        def load_words(name, words, queue, tag=None):
-            raw = sbuf(name, [P, 2 * FEATURES], U8, tag)
-            queue.dma_start(raw[:].bitcast(I32), words[0].bitcast(I32))
-            return raw
+        def load_words(queue, raw, words):
+            queue.dma_start(raw.bitcast(I32), words[0].bitcast(I32))
 
         def deal_words(name, raw, tag=None):
             dealt = sbuf(name, [P, 2 * FEATURES], U8, tag)
             nc.vector.tensor_copy(
                 dealt[:].rearrange("p (t m b) -> p t m b", t=PACK, b=2),
-                raw[:].rearrange("p (m t b) -> p t m b", t=PACK, b=2),
+                raw.rearrange("p (m t b) -> p t m b", t=PACK, b=2),
             )
             return dealt
 
@@ -86,7 +85,7 @@ def tile_picked_twlflowbgsumg_none_po_kernel(
             dealt = sbuf(name, [P, FEATURES], U8, tag)
             nc.vector.tensor_copy(
                 dealt[:].rearrange("p (t m) -> p t m", t=PACK),
-                raw[:].rearrange("p (m t) -> p t m", t=PACK),
+                raw.rearrange("p (m t) -> p t m", t=PACK),
             )
             return dealt
 
@@ -110,10 +109,15 @@ def tile_picked_twlflowbgsumg_none_po_kernel(
         warm_out = sbuf("warm_out", [P, 1], F32)
         nc.gpsimd.memset(warm_in[:], 0.0)
         nc.scalar.activation(warm_out[:], warm_in[:], SIGMOID)
-        w1_plane = zeroed_plane("w1_plane", FEATURES)
         x_plane = zeroed_plane("x_plane", T)
+        w1_plane = zeroed_plane("w1_plane", FEATURES)
         w2_plane = zeroed_plane("w2_plane", FEATURES)
-        w1_raw = load_words("w1_raw", w1_words, nc.sync)
+        w3_plane = zeroed_plane("w3_plane", FEATURES)
+        d_rows = [window(f"d_rows{t}") for t in range(PACK)]
+        y_rows = [window(f"y_rows{t}") for t in range(PACK)]
+        h_rows = [window(f"h_rows{t}") for t in range(PACK)]
+        w1_raw = sbuf("w1_raw", [P, 2 * FEATURES], U8, "raw_words")
+        load_words(nc.sync, w1_raw[:], w1_words)
         offs_t = load_list("offs_t", offs)
         two_t = load_list("two_t", two)
         n1_t = load_list("n1_t", n1)
@@ -122,33 +126,31 @@ def tile_picked_twlflowbgsumg_none_po_kernel(
         n4_t = load_list("n4_t", n4)
         x_table = sbuf("x_table", [P, T], U32)
         nc.sync.dma_start(x_table[:].bitcast(I32), x_words[0].rearrange("p c r -> p (c r)").bitcast(I32))
-        load_scale_rows([nc.scalar] * 3 + [nc.gpsimd], w1_plane, w1_scales)
-        load_scale_rows([nc.scalar] * 4, x_plane, x_scales)
-        load_scale_rows([nc.scalar] * 4, w2_plane, w2_scales)
-        w2_raw = load_words("w2_raw", w2_words, nc.gpsimd)
-        gain = sbuf("gain", [P, PACK], F32)
-        nc.gpsimd.dma_start(gain[:], gn.rearrange("(p t) o -> p (t o)", t=PACK))
+        load_scale_rows([nc.sync] * 3 + [nc.gpsimd], x_plane, x_scales[0])
+        load_scale_rows([nc.sync] * 4, w1_plane, w1_scales[0])
+        load_scale_rows([nc.sync] * 4, w2_plane, w2_scales[0])
+        gain = d_rows[PACK - 1][:, S : S + PACK]
+        nc.sync.dma_start(gain, gn.rearrange("(p t) o -> p (t o)", t=PACK))
+        load_scale_rows([nc.sync] * 4, w3_plane, w3_scales[0])
 
-        y_rows = [window(f"y_rows{t}") for t in range(PACK)]
-        d_rows = [window(f"d_rows{t}") for t in range(PACK)]
-        h_rows = [window(f"h_rows{t}") for t in range(PACK)]
+        w1_dealt = deal_words("w1_dealt", w1_raw[:])
+        w2_raw = sbuf("w2_raw", [P, 2 * FEATURES], U8, "raw_words")
+        load_words(nc.gpsimd, w2_raw[:], w2_words)
 
-        w1_dealt = deal_words("w1_dealt", w1_raw)
-        w1_sdealt = deal_scales("w1_sdealt", w1_plane)
-        w2_dealt = deal_words("w2_dealt", w2_raw)
-        w3_raw = load_words("w3_raw", w3_words, nc.sync, "w1_raw")
-        load_scale_rows([nc.sync] * 4, w1_plane, w3_scales)
+        def pick(name, dtype, table, offsets, tag=None):
+            picked = sbuf(name, [P, S], dtype, tag)
+            nc.vector.tensor_copy(picked[:], table[:].indirect(offsets[:]))
+            return picked
 
-        def pick(name, offsets):
-            codes = sbuf(name + "_codes", [P, S], U32)
-            code_scales = sbuf(name + "_scales", [P, S], U8)
-            nc.vector.tensor_copy(codes[:], x_table[:].indirect(offsets[:]))
-            nc.vector.tensor_copy(code_scales[:], x_plane[:].indirect(offsets[:]))
-            return codes, code_scales
-
-        xq_codes, xq_scales = pick("xq", offs_t)
-        w2_sdealt = deal_scales("w2_sdealt", w2_plane)
-        x2_codes, x2_scales = pick("x2", two_t)
+        xq_codes = pick("xq_codes", U32, x_table, offs_t)
+        x2_codes = pick("x2_codes", U32, x_table, two_t)
+        xq_scales = pick("xq_scales", U8, x_plane, offs_t)
+        w1_sdealt = deal_scales("w1_sdealt", w1_plane[:])
+        x2_scales = pick("x2_scales", U8, x_plane, two_t, "w1_plane")
+        w2_dealt = deal_words("w2_dealt", w2_raw[:], "x_plane")
+        w2_sdealt = deal_scales("w2_sdealt", w2_plane[:], "raw_words")
+        w3_raw = sbuf("w3_raw", [P, 2 * FEATURES], U8, "x_table")
+        load_words(nc.sync, w3_raw[:], w3_words)
 
         banks = [bank(f"yd_bank{t}") for t in range(PACK + 1)]
         y_sums = [banks[t][:, :S] for t in range(PACK)]
@@ -158,7 +160,6 @@ def tile_picked_twlflowbgsumg_none_po_kernel(
         for t in range(PACK):
             product(d_sums[t], w2_dealt, w2_sdealt, t, x2_codes[:], x2_scales[:])
 
-        first = sbuf("first", [P, PACK, S], F32)
         second = sbuf("second", [P, PACK, S], F32)
         pieces = [(t, 0, S) for t in range(PACK - 1)] + [(PACK - 1, 0, HALF), (PACK - 1, HALF, S)]
         fetched, steps, d_fetched = {}, {}, {}
@@ -167,10 +168,10 @@ def tile_picked_twlflowbgsumg_none_po_kernel(
             return offsets[:, c0 // LIST_ROWS : c1 // LIST_ROWS]
 
         def y_out(t):
-            nc.scalar.activation(y_rows[t][:, :S], y_sums[t], COPY, scale=gain[:, t : t + 1])
+            nc.scalar.activation(y_rows[t][:, :S], y_sums[t], COPY, scale=0.5)
 
         def d_out(t):
-            nc.scalar.activation(d_rows[t][:, :S], d_sums[t], COPY, scale=0.5)
+            nc.scalar.activation(d_rows[t][:, :S], d_sums[t], COPY, scale=gain[:, t : t + 1])
 
         def fetch_y(i):
             t, c0, c1 = pieces[i]
@@ -185,7 +186,7 @@ def tile_picked_twlflowbgsumg_none_po_kernel(
 
         def differences(i):
             t, c0, c1 = pieces[i]
-            steps[i] = sbuf(f"steps{i}", [P, 2, c1 - c0], F32)
+            steps[i] = sbuf(f"steps{i}", [P, 2, c1 - c0], F32, {0: "w2_plane", 1: "w3_plane"}.get(i))
             here = y_rows[t][:, c0:c1].unsqueeze(1).to_broadcast([P, 2, c1 - c0])
             nc.vector.tensor_tensor(steps[i][:], fetched[i][:], here, SUBTRACT)
 
@@ -211,9 +212,11 @@ def tile_picked_twlflowbgsumg_none_po_kernel(
 
         y_out(0)
         fetch_y(0)
-        d_out(0)
         differences(0)
-        w3_dealt = deal_words("w3_dealt", w3_raw, "fetched0")
+        d_out(0)
+        w3_dealt = deal_words("w3_dealt", w3_raw[:], "fetched0")
+        w3_sdealt = deal_scales("w3_sdealt", w3_plane[:], "xq_scales")
+        first = sbuf("first", [P, PACK, S], F32, "x_table")
         for i in range(1, len(pieces)):
             t, c0, c1 = pieces[i]
             if c0 == 0:
@@ -225,22 +228,21 @@ def tile_picked_twlflowbgsumg_none_po_kernel(
             first_term(i - 1)
             second_term(i - 1)
             differences(i)
-            if i == 1:
-                w3_sdealt = deal_scales("w3_sdealt", w1_plane, "fetched1")
 
-        h_banks = {}
+        h_banks, h_sums = {}, {}
 
         def last_layer(u):
             codes = sbuf(f"z_codes{u}", [P, HALF], U32)
             code_scales = sbuf(f"z_scales{u}", [P, HALF], U8)
             nc.vector.quantize_mx(codes[:].bitcast(FP8X4), code_scales[:], z_grouped[u][:].rearrange("p c t -> p (c t)"))
-            for pair in range(2):
-                h_banks[u, pair] = bank(f"h_bank{u}_{pair}")
-                for t in (2 * pair, 2 * pair + 1):
-                    product(h_banks[u, pair][:, HALF * (t % 2) : HALF * (t % 2 + 1)], w3_dealt, w3_sdealt, t, codes[:], code_scales[:])
+            for t0, t1 in BANK_TILES[u]:
+                h_banks[u, t0] = bank(f"h_bank{u}_{t0}")
+                for t in range(t0, t1):
+                    h_sums[u, t] = h_banks[u, t0][:, HALF * (t - t0) : HALF * (t - t0 + 1)]
+                    product(h_sums[u, t], w3_dealt, w3_sdealt, t, codes[:], code_scales[:])
             for t in range(PACK):
                 copy = nc.vector.tensor_copy if u == 1 and t < 2 else nc.scalar.copy
-                copy(h_rows[t][:, HALF * u : HALF * (u + 1)], h_banks[u, t // 2][:, HALF * (t % 2) : HALF * (t % 2 + 1)])
+                copy(h_rows[t][:, HALF * u : HALF * (u + 1)], h_sums[u, t])
 
         join(0)
         first_term(len(pieces) - 1)
@@ -286,14 +288,9 @@ def tile_picked_twlflowbgsumg_none_po_kernel(
             c0, c1 = CHUNKS[k]
             g0, g1 = group_of(k)
             u = c0 // HALF
-            for pair in range(2):
-                h_here = h_banks[u, pair][:, :S].rearrange("p (t c) -> p t c", t=2)
-                nc.vector.tensor_tensor(
-                    results[g0][:, 2 * pair : 2 * pair + 2, c0 - g0 : c1 - g0],
-                    h_here[:, :, c0 - HALF * u : c1 - HALF * u],
-                    gates[k][:, 2 * pair : 2 * pair + 2, :],
-                    MULT,
-                )
+            for t0, t1 in BANK_TILES[u]:
+                h_here = h_banks[u, t0][:].rearrange("p (t c) -> p t c", c=HALF)[:, : t1 - t0, c0 - HALF * u : c1 - HALF * u]
+                nc.vector.tensor_tensor(results[g0][:, t0:t1, c0 - g0 : c1 - g0], h_here, gates[k][:, t0:t1, :], MULT)
             if c1 == g1:
                 nc.sync.dma_start(out_rows[:, :, g0:g1], results[g0][:])
 

@@ -1,6 +1,7 @@
 from contextlib import ExitStack
 
 import concourse.mybir as mybir
+from concourse.masks import make_identity
 
 F32 = mybir.dt.float32
 BF16 = mybir.dt.bfloat16
@@ -27,9 +28,9 @@ LIST_ROWS = 16
 SPARE = 16
 FLOPS = 3 * 2 * FEATURES * FEATURES * S
 
-CHUNKS = ((0, 64), (64, 128), (128, 192), (192, 224), (224, 256))
+CHUNKS = ((128, 192), (192, 224), (224, 256))
 QUANT_GROUPS = ((0, 128), (128, 192), (192, 256))
-VECTOR_GATHERS = (2, 2, 1, 0, 0)
+VECTOR_GATHERS = (2, 0, 0)
 BANK_TILES = (((0, 4),), ((0, 2), (2, 4)))
 
 
@@ -109,6 +110,8 @@ def tile_picked_twlflowbgsumg_none_po_kernel(
         warm_out = sbuf("warm_out", [P, 1], F32)
         nc.gpsimd.memset(warm_in[:], 0.0)
         nc.scalar.activation(warm_out[:], warm_in[:], SIGMOID)
+        identity = sbuf("identity", [P, P], F32)
+        make_identity(nc, identity[:])
         x_plane = zeroed_plane("x_plane", T)
         w1_plane = zeroed_plane("w1_plane", FEATURES)
         w2_plane = zeroed_plane("w2_plane", FEATURES)
@@ -223,7 +226,7 @@ def tile_picked_twlflowbgsumg_none_po_kernel(
                 y_out(t)
                 d_out(t)
             fetch_y(i)
-            if t == PACK - 1:
+            if t >= PACK - 2:
                 fetch_d(i)
             first_term(i - 1)
             second_term(i - 1)
@@ -260,7 +263,7 @@ def tile_picked_twlflowbgsumg_none_po_kernel(
 
         def fetch_members(k):
             c0, c1 = CHUNKS[k]
-            members[k] = sbuf(f"members{k}", [P, PACK, MEMBERS * (c1 - c0)], F32)
+            members[k] = sbuf(f"members{k}", [P, PACK, MEMBERS * (c1 - c0)], F32, "low_members3" if k == 2 else None)
             for t in range(PACK):
                 looked_up = h_rows[t][:].indirect(entries(n4_t, MEMBERS * c0, MEMBERS * c1))
                 if t < VECTOR_GATHERS[k]:
@@ -284,46 +287,70 @@ def tile_picked_twlflowbgsumg_none_po_kernel(
         def group_of(k):
             return [g for g in QUANT_GROUPS if g[0] <= CHUNKS[k][0] < g[1]][0]
 
+        def store_result(g0, g1):
+            nc.sync.dma_start(out_rows[:, :, g0:g1], results[g0][:])
+
         def multiply(k):
             c0, c1 = CHUNKS[k]
             g0, g1 = group_of(k)
-            u = c0 // HALF
-            for t0, t1 in BANK_TILES[u]:
-                h_here = h_banks[u, t0][:].rearrange("p (t c) -> p t c", c=HALF)[:, : t1 - t0, c0 - HALF * u : c1 - HALF * u]
+            for t0, t1 in BANK_TILES[1]:
+                h_here = h_banks[1, t0][:].rearrange("p (t c) -> p t c", c=HALF)[:, : t1 - t0, c0 - HALF : c1 - HALF]
                 nc.vector.tensor_tensor(results[g0][:, t0:t1, c0 - g0 : c1 - g0], h_here, gates[k][:, t0:t1, :], MULT)
             if c1 == g1:
-                nc.sync.dma_start(out_rows[:, :, g0:g1], results[g0][:])
+                store_result(g0, g1)
 
-        def regroup(k):
-            g0, g1 = group_of(k)
-            if CHUNKS[k][1] == g1:
-                interleave(nc.vector.tensor_copy, grouped[g0][:], results[g0][:])
+        def regroup(g0):
+            interleave(nc.vector.tensor_copy, grouped[g0][:], results[g0][:])
 
-        def quantise(k):
-            g0, g1 = group_of(k)
-            if CHUNKS[k][1] == g1:
-                codes = sbuf(f"out_codes{g0}", [P, g1 - g0], U32)
-                nc.vector.quantize_mx(codes[:].bitcast(FP8X4), out_plane[:, g0:g1], grouped[g0][:].rearrange("p c t -> p (c t)"))
-                nc.sync.dma_start(out_words[:, g0:g1], codes[:].bitcast(I32))
+        def quantise(g0, g1):
+            codes = sbuf(f"out_codes{g0}", [P, g1 - g0], U32)
+            nc.vector.quantize_mx(codes[:].bitcast(FP8X4), out_plane[:, g0:g1], grouped[g0][:].rearrange("p c t -> p (c t)"))
+            nc.sync.dma_start(out_words[:, g0:g1], codes[:].bitcast(I32))
 
-        last = len(CHUNKS) - 1
+        low_members = [sbuf(f"low_members{t}", [P, MEMBERS * HALF], F32) for t in range(PACK)]
+        turned_sums = bank("turned_sums")
+        for t in (0, 2, 1, 3):
+            for e0 in range(0, MEMBERS * HALF, S):
+                looked_up = h_rows[t][:].indirect(entries(n4_t, e0, e0 + S))
+                if t < 2:
+                    nc.vector.tensor_copy(low_members[t][:, e0 : e0 + S], looked_up)
+                else:
+                    nc.scalar.activation(low_members[t][:, e0 : e0 + S], looked_up, COPY)
+            for f in range(MEMBERS):
+                nc.tensor.matmul(
+                    turned_sums[:, P * t : P * (t + 1)],
+                    lhsT=low_members[t][:, f::MEMBERS],
+                    rhs=identity[:],
+                    is_transpose=True,
+                    start=f == 0,
+                    stop=f == MEMBERS - 1,
+                )
         fetch_members(0)
+        add_pairs(0)
         fetch_members(1)
-        for k in range(len(CHUNKS)):
-            add_pairs(k)
-            if k >= 2:
-                quantise(k - 2)
-            if k + 2 <= last:
-                fetch_members(k + 2)
-            if k >= 1:
-                multiply(k - 1)
-            gate(k)
-            if k >= 1:
-                regroup(k - 1)
-        quantise(last - 1)
-        multiply(last)
-        regroup(last)
-        quantise(last)
+        turned_gates = sbuf("turned_gates", [P, PACK * P], F32)
+        nc.scalar.activation(turned_gates[:], turned_sums[:], SIGMOID)
+        low_gates = bank("low_gates")
+        for t in range(PACK):
+            nc.tensor.transpose(low_gates[:, P * t : P * (t + 1)], turned_gates[:, P * t : P * (t + 1)], identity[:])
+        gate(0)
+        fetch_members(2)
+        add_pairs(1)
+        for t in range(PACK):
+            nc.vector.tensor_tensor(results[0][:, t, :], low_gates[:, P * t : P * (t + 1)], h_rows[t][:, :HALF], MULT)
+        store_result(*QUANT_GROUPS[0])
+        gate(1)
+        regroup(0)
+        multiply(0)
+        quantise(*QUANT_GROUPS[0])
+        add_pairs(2)
+        regroup(QUANT_GROUPS[1][0])
+        gate(2)
+        multiply(1)
+        quantise(*QUANT_GROUPS[1])
+        multiply(2)
+        regroup(QUANT_GROUPS[2][0])
+        quantise(*QUANT_GROUPS[2])
         for q in range(4):
             queue = nc.scalar if q % 2 else nc.sync
             queue.dma_start(out_2[0, 4 * q : 4 * q + 4, :].bitcast(I32), out_plane[32 * q : 32 * q + 4, :].bitcast(I32))

from contextlib import ExitStack

import concourse.mybir as mybir
from concourse.masks import make_identity

F32 = mybir.dt.float32
BF16 = mybir.dt.bfloat16
I32 = mybir.dt.int32
U32 = mybir.dt.uint32
U16 = mybir.dt.uint16
U8 = mybir.dt.uint8
FP8X4 = mybir.dt.float8_e4m3fn_x4
FP4X4 = mybir.dt.float4_e2m1fn_x4
MULT = mybir.AluOpType.mult
ADD = mybir.AluOpType.add
SUBTRACT = mybir.AluOpType.subtract
COPY = mybir.ActivationFunctionType.Copy
SIGMOID = mybir.ActivationFunctionType.Sigmoid

P = 128
PACK = 4
T = 2048
S = 256
HALF = S // 2
FEATURES = P * PACK
MEMBERS = 4
LIST_ROWS = 16
SPARE = 16
FLOPS = 3 * 2 * FEATURES * FEATURES * S

CHUNKS = ((128, 192), (192, 224), (224, 256))
QUANT_GROUPS = ((0, 128), (128, 192), (192, 256))
VECTOR_GATHERS = (2, 0, 0)
BANK_TILES = (((0, 4),), ((0, 2), (2, 4)))


def load_scale_rows(queues, plane, scales):
    for q, queue in enumerate(queues):
        queue.dma_start(plane[32 * q : 32 * q + 4, :].bitcast(I32), scales[4 * q : 4 * q + 4, :].bitcast(I32))


def interleave(copy, grouped, rows):
    copy(
        grouped.rearrange("p (c i) t -> p c t i", i=4),
        rows.rearrange("p t (c i) -> p c t i", i=4),
    )


def tile_picked_twlflowbgsumg_none_po_kernel(
    tc, x_words, x_scales, w1_words, w1_scales, w2_words, w2_scales, gn, w3_words, w3_scales,
    offs, two, n1, n2, n3, n4, out_0, out_1, out_2,
):
    nc = tc.nc
    with ExitStack() as ctx:
        keep = ctx.enter_context(tc.tile_pool(name="keep", bufs=1))
        psum = ctx.enter_context(tc.psum_pool(name="psum", bufs=8))

        def sbuf(name, shape, dtype, tag=None):
            return keep.tile(shape, dtype, name=name, tag=tag or name, align_bytes=64)

        def bank(name):
            return psum.tile([P, 512], F32, name=name, tag="bank")

        def load_list(name, source):
            tile = sbuf(name, list(source.shape), U16)
            nc.sync.dma_start(tile[:], source)
            return tile

        def zeroed_plane(name, width):
            plane = sbuf(name, [P, width], U8)
            nc.vector.memset(plane[:].bitcast(I32), 0)
            return plane

        def load_words(queue, raw, words):
            queue.dma_start(raw.bitcast(I32), words[0].bitcast(I32))

        def deal_words(name, raw, tag=None):
            dealt = sbuf(name, [P, 2 * FEATURES], U8, tag)
            nc.vector.tensor_copy(
                dealt[:].rearrange("p (t m b) -> p t m b", t=PACK, b=2),
                raw.rearrange("p (m t b) -> p t m b", t=PACK, b=2),
            )
            return dealt

        def deal_scales(name, raw, tag=None):
            dealt = sbuf(name, [P, FEATURES], U8, tag)
            nc.vector.tensor_copy(
                dealt[:].rearrange("p (t m) -> p t m", t=PACK),
                raw.rearrange("p (m t) -> p t m", t=PACK),
            )
            return dealt

        def window(name):
            tile = sbuf(name, [P, S + SPARE], F32)
            nc.vector.memset(tile[:, S:], 0.0)
            return tile

        def product(out, words, scales, t, codes, code_scales):
            nc.tensor.matmul_mx(
                out,
                lhsT=words[:, 2 * P * t : 2 * P * (t + 1)].bitcast(FP4X4),
                lhsT_scale=scales[:, P * t : P * (t + 1)],
                rhs=codes.bitcast(FP8X4),
                rhs_scale=code_scales,
                start=True,
                stop=True,
            )

        warm_in = sbuf("warm_in", [P, 1], F32)
        warm_out = sbuf("warm_out", [P, 1], F32)
        nc.gpsimd.memset(warm_in[:], 0.0)
        nc.scalar.activation(warm_out[:], warm_in[:], SIGMOID)
        identity = sbuf("identity", [P, P], F32)
        make_identity(nc, identity[:])
        x_plane = zeroed_plane("x_plane", T)
        w1_plane = zeroed_plane("w1_plane", FEATURES)
        w2_plane = zeroed_plane("w2_plane", FEATURES)
        w3_plane = zeroed_plane("w3_plane", FEATURES)
        d_rows = [window(f"d_rows{t}") for t in range(PACK)]
        y_rows = [window(f"y_rows{t}") for t in range(PACK)]
        h_rows = [window(f"h_rows{t}") for t in range(PACK)]
        w1_raw = sbuf("w1_raw", [P, 2 * FEATURES], U8, "raw_words")
        load_words(nc.sync, w1_raw[:], w1_words)
        offs_t = load_list("offs_t", offs)
        two_t = load_list("two_t", two)
        n1_t = load_list("n1_t", n1)
        n2_t = load_list("n2_t", n2)
        n3_t = load_list("n3_t", n3)
        n4_t = load_list("n4_t", n4)
        x_table = sbuf("x_table", [P, T], U32)
        nc.sync.dma_start(x_table[:].bitcast(I32), x_words[0].rearrange("p c r -> p (c r)").bitcast(I32))
        load_scale_rows([nc.sync] * 3 + [nc.gpsimd], x_plane, x_scales[0])
        load_scale_rows([nc.sync] * 4, w1_plane, w1_scales[0])
        load_scale_rows([nc.sync] * 4, w2_plane, w2_scales[0])
        gain = d_rows[PACK - 1][:, S : S + PACK]
        nc.sync.dma_start(gain, gn.rearrange("(p t) o -> p (t o)", t=PACK))
        load_scale_rows([nc.sync] * 4, w3_plane, w3_scales[0])

        w1_dealt = deal_words("w1_dealt", w1_raw[:])
        w2_raw = sbuf("w2_raw", [P, 2 * FEATURES], U8, "raw_words")
        load_words(nc.gpsimd, w2_raw[:], w2_words)

        def pick(name, dtype, table, offsets, tag=None):
            picked = sbuf(name, [P, S], dtype, tag)
            nc.vector.tensor_copy(picked[:], table[:].indirect(offsets[:]))
            return picked

        xq_codes = pick("xq_codes", U32, x_table, offs_t)
        x2_codes = pick("x2_codes", U32, x_table, two_t)
        xq_scales = pick("xq_scales", U8, x_plane, offs_t)
        w1_sdealt = deal_scales("w1_sdealt", w1_plane[:])
        x2_scales = pick("x2_scales", U8, x_plane, two_t, "w1_plane")
        w2_dealt = deal_words("w2_dealt", w2_raw[:], "x_plane")
        w2_sdealt = deal_scales("w2_sdealt", w2_plane[:], "raw_words")
        w3_raw = sbuf("w3_raw", [P, 2 * FEATURES], U8, "x_table")
        load_words(nc.sync, w3_raw[:], w3_words)

        banks = [bank(f"yd_bank{t}") for t in range(PACK + 1)]
        y_sums = [banks[t][:, :S] for t in range(PACK)]
        d_sums = [banks[t + 1][:, S:] for t in range(PACK)]
        for t in range(PACK):
            product(y_sums[t], w1_dealt, w1_sdealt, t, xq_codes[:], xq_scales[:])
        for t in range(PACK):
            product(d_sums[t], w2_dealt, w2_sdealt, t, x2_codes[:], x2_scales[:])

        second = sbuf("second", [P, PACK, S], F32)
        pieces = [(t, 0, S) for t in range(PACK - 1)] + [(PACK - 1, 0, HALF), (PACK - 1, HALF, S)]
        fetched, steps, d_fetched = {}, {}, {}

        def entries(offsets, c0, c1):
            return offsets[:, c0 // LIST_ROWS : c1 // LIST_ROWS]

        def y_out(t):
            nc.scalar.activation(y_rows[t][:, :S], y_sums[t], COPY, scale=0.5)

        def d_out(t):
            nc.scalar.activation(d_rows[t][:, :S], d_sums[t], COPY, scale=gain[:, t : t + 1])

        def fetch_y(i):
            t, c0, c1 = pieces[i]
            fetched[i] = sbuf(f"fetched{i}", [P, 2, c1 - c0], F32)
            nc.scalar.activation(fetched[i][:, 0, :], y_rows[t][:].indirect(entries(n1_t, c0, c1)), COPY)
            nc.scalar.activation(fetched[i][:, 1, :], y_rows[t][:].indirect(entries(n2_t, c0, c1)), COPY)

        def fetch_d(i):
            t, c0, c1 = pieces[i]
            d_fetched[i] = sbuf(f"d_fetched{i}", [P, c1 - c0], F32)
            nc.scalar.activation(d_fetched[i][:], d_rows[t][:].indirect(entries(n3_t, c0, c1)), COPY)

        def differences(i):
            t, c0, c1 = pieces[i]
            steps[i] = sbuf(f"steps{i}", [P, 2, c1 - c0], F32, {0: "w2_plane", 1: "w3_plane"}.get(i))
            here = y_rows[t][:, c0:c1].unsqueeze(1).to_broadcast([P, 2, c1 - c0])
            nc.vector.tensor_tensor(steps[i][:], fetched[i][:], here, SUBTRACT)

        def first_term(i):
            t, c0, c1 = pieces[i]
            nc.vector.scalar_tensor_tensor(first[:, t, c0:c1], steps[i][:, 0, :], 2.0, d_rows[t][:, c0:c1], MULT, MULT)

        def second_term(i):
            t, c0, c1 = pieces[i]
            d_there = d_fetched[i][:] if i in d_fetched else d_rows[t][:].indirect(entries(n3_t, c0, c1))
            nc.vector.tensor_tensor(second[:, t, c0:c1], d_there, steps[i][:, 1, :], MULT)

        z_grouped = [sbuf(f"z_grouped{u}", [P, HALF, PACK], BF16) for u in range(2)]

        def join(u):
            cols = slice(HALF * u, HALF * (u + 1))
            nc.vector.tensor_tensor(
                z_grouped[u][:].rearrange("p (c i) t -> p c t i", i=4),
                first[:, :, cols].rearrange("p t (c i) -> p c t i", i=4),
                second[:, :, cols].rearrange("p t (c i) -> p c t i", i=4),
                ADD,
            )

        y_out(0)
        fetch_y(0)
        differences(0)
        d_out(0)
        w3_dealt = deal_words("w3_dealt", w3_raw[:], "fetched0")
        w3_sdealt = deal_scales("w3_sdealt", w3_plane[:], "xq_scales")
        first = sbuf("first", [P, PACK, S], F32, "x_table")
        for i in range(1, len(pieces)):
            t, c0, c1 = pieces[i]
            if c0 == 0:
                y_out(t)
                d_out(t)
            fetch_y(i)
            if t >= PACK - 2:
                fetch_d(i)
            first_term(i - 1)
            second_term(i - 1)
            differences(i)

        h_banks, h_sums = {}, {}

        def last_layer(u):
            codes = sbuf(f"z_codes{u}", [P, HALF], U32)
            code_scales = sbuf(f"z_scales{u}", [P, HALF], U8)
            nc.vector.quantize_mx(codes[:].bitcast(FP8X4), code_scales[:], z_grouped[u][:].rearrange("p c t -> p (c t)"))
            for t0, t1 in BANK_TILES[u]:
                h_banks[u, t0] = bank(f"h_bank{u}_{t0}")
                for t in range(t0, t1):
                    h_sums[u, t] = h_banks[u, t0][:, HALF * (t - t0) : HALF * (t - t0 + 1)]
                    product(h_sums[u, t], w3_dealt, w3_sdealt, t, codes[:], code_scales[:])
            for t in range(PACK):
                copy = nc.vector.tensor_copy if u == 1 and t < 2 else nc.scalar.copy
                copy(h_rows[t][:, HALF * u : HALF * (u + 1)], h_sums[u, t])

        join(0)
        first_term(len(pieces) - 1)
        second_term(len(pieces) - 1)
        last_layer(0)
        join(1)
        last_layer(1)

        out_rows = out_0.rearrange("(p t) c -> p t c", t=PACK)
        out_words = out_1[0].rearrange("p c r -> p (c r)").bitcast(I32)
        out_plane = sbuf("out_plane", [P, S], U8)
        results = {g0: sbuf(f"result{g0}", [P, PACK, g1 - g0], F32) for g0, g1 in QUANT_GROUPS}
        grouped = {g0: sbuf(f"out_grouped{g0}", [P, g1 - g0, PACK], BF16) for g0, g1 in QUANT_GROUPS}
        members, pairs, sums, gates = {}, {}, {}, {}

        def fetch_members(k):
            c0, c1 = CHUNKS[k]
            members[k] = sbuf(f"members{k}", [P, PACK, MEMBERS * (c1 - c0)], F32, "low_members3" if k == 2 else None)
            for t in range(PACK):
                looked_up = h_rows[t][:].indirect(entries(n4_t, MEMBERS * c0, MEMBERS * c1))
                if t < VECTOR_GATHERS[k]:
                    nc.vector.tensor_copy(members[k][:, t, :], looked_up)
                else:
                    nc.scalar.activation(members[k][:, t, :], looked_up, COPY)

        def add_pairs(k):
            c0, c1 = CHUNKS[k]
            fours = members[k][:].rearrange("p t (c f) -> p (t c) f", f=MEMBERS)
            pairs[k] = sbuf(f"pairs{k}", [P, PACK * (c1 - c0), 2], F32)
            nc.vector.tensor_tensor(pairs[k][:], fours[:, :, 0:2], fours[:, :, 2:4], ADD)

        def gate(k):
            c0, c1 = CHUNKS[k]
            sums[k] = sbuf(f"sums{k}", [P, PACK * (c1 - c0)], F32)
            gates[k] = sbuf(f"gates{k}", [P, PACK, c1 - c0], F32)
            nc.vector.tensor_tensor(sums[k][:], pairs[k][:, :, 0], pairs[k][:, :, 1], ADD)
            nc.scalar.activation(gates[k][:].rearrange("p t c -> p (t c)"), sums[k][:], SIGMOID)

        def group_of(k):
            return [g for g in QUANT_GROUPS if g[0] <= CHUNKS[k][0] < g[1]][0]

        def store_result(g0, g1):
            nc.sync.dma_start(out_rows[:, :, g0:g1], results[g0][:])

        def multiply(k):
            c0, c1 = CHUNKS[k]
            g0, g1 = group_of(k)
            for t0, t1 in BANK_TILES[1]:
                h_here = h_banks[1, t0][:].rearrange("p (t c) -> p t c", c=HALF)[:, : t1 - t0, c0 - HALF : c1 - HALF]
                nc.vector.tensor_tensor(results[g0][:, t0:t1, c0 - g0 : c1 - g0], h_here, gates[k][:, t0:t1, :], MULT)
            if c1 == g1:
                store_result(g0, g1)

        def regroup(g0):
            interleave(nc.vector.tensor_copy, grouped[g0][:], results[g0][:])

        def quantise(g0, g1):
            codes = sbuf(f"out_codes{g0}", [P, g1 - g0], U32)
            nc.vector.quantize_mx(codes[:].bitcast(FP8X4), out_plane[:, g0:g1], grouped[g0][:].rearrange("p c t -> p (c t)"))
            nc.sync.dma_start(out_words[:, g0:g1], codes[:].bitcast(I32))

        low_members = [sbuf(f"low_members{t}", [P, MEMBERS * HALF], F32) for t in range(PACK)]
        turned_sums = bank("turned_sums")
        for t in (0, 2, 1, 3):
            for e0 in range(0, MEMBERS * HALF, S):
                looked_up = h_rows[t][:].indirect(entries(n4_t, e0, e0 + S))
                if t < 2:
                    nc.vector.tensor_copy(low_members[t][:, e0 : e0 + S], looked_up)
                else:
                    nc.scalar.activation(low_members[t][:, e0 : e0 + S], looked_up, COPY)
            for f in range(MEMBERS):
                nc.tensor.matmul(
                    turned_sums[:, P * t : P * (t + 1)],
                    lhsT=low_members[t][:, f::MEMBERS],
                    rhs=identity[:],
                    is_transpose=True,
                    start=f == 0,
                    stop=f == MEMBERS - 1,
                )
        fetch_members(0)
        add_pairs(0)
        fetch_members(1)
        turned_gates = sbuf("turned_gates", [P, PACK * P], F32)
        nc.scalar.activation(turned_gates[:], turned_sums[:], SIGMOID)
        low_gates = bank("low_gates")
        for t in range(PACK):
            nc.tensor.transpose(low_gates[:, P * t : P * (t + 1)], turned_gates[:, P * t : P * (t + 1)], identity[:])
        gate(0)
        fetch_members(2)
        add_pairs(1)
        for t in range(PACK):
            nc.vector.tensor_tensor(results[0][:, t, :], low_gates[:, P * t : P * (t + 1)], h_rows[t][:, :HALF], MULT)
        store_result(*QUANT_GROUPS[0])
        gate(1)
        regroup(0)
        multiply(0)
        quantise(*QUANT_GROUPS[0])
        add_pairs(2)
        regroup(QUANT_GROUPS[1][0])
        gate(2)
        multiply(1)
        quantise(*QUANT_GROUPS[1])
        multiply(2)
        regroup(QUANT_GROUPS[2][0])
        quantise(*QUANT_GROUPS[2])
        for q in range(4):
            queue = nc.scalar if q % 2 else nc.sync
            queue.dma_start(out_2[0, 4 * q : 4 * q + 4, :].bitcast(I32), out_plane[32 * q : 32 * q + 4, :].bitcast(I32))
